import numpy as np
import ml_dtypes


def mxq(x, axis, fmt="e4m3"):
    dtype, down = {"e4m3": (ml_dtypes.float8_e4m3fn, 7), "e5m2": (ml_dtypes.float8_e5m2, 14)}[fmt]
    v = np.moveaxis(np.asarray(x, np.float32).astype(ml_dtypes.bfloat16).astype(np.float64), axis, -1)
    blocks = v.reshape(v.shape[:-1] + (-1, 32))
    amax = np.abs(blocks).max(-1, keepdims=True)
    byte = np.maximum(np.where(amax > 0, np.frexp(amax)[1] - 1 + 127, 0) - down, 1)
    scale = np.exp2(byte - 127.0)
    codes = (blocks / scale).astype(np.float32).astype(dtype).astype(np.float64)
    return np.moveaxis((codes * scale).reshape(v.shape), -1, axis)


WIDE = False


def mx_kscale(k):
    if not WIDE:
        return np.ones(k)
    levels = np.array([10, -10, 5, -5, 0])
    if k % 512:
        return np.exp2(np.random.permutation(np.resize(levels, k // 32))).repeat(32)
    a = np.empty((k // 512, 16))
    for p in range(k // 512):
        a[p, :8] = np.random.permutation(np.resize(levels, 8))
        for g in range(8):
            far = levels[np.abs(levels - a[p, g]) >= 10]
            a[p, g + 8] = far[np.random.randint(len(far))]
    return np.exp2(a.ravel()).repeat(32)


def f64(x):
    return np.asarray(x).astype(np.float64)


def striped(idx):
    return np.tile(np.asarray(idx).reshape(-1, 16).T, (8, 1)).astype(np.uint16)


def unstriped(offs):
    return offs[:16].T.reshape(-1).astype(np.int64)


E2M1 = np.array([0.0, 0.5, 1.0, 1.5, 2.0, 3.0, 4.0, 6.0, -0.0, -0.5, -1.0, -1.5, -2.0, -3.0, -4.0, -6.0])


def pack_weight(w, fmt):
    k, n = w.shape
    w = f64(np.asarray(w, np.float32).astype(ml_dtypes.bfloat16)).reshape(k // 32, 32, n)
    amax = np.abs(w).max(1)
    if fmt == "e4m3":
        byte = np.frexp(amax)[1] - 1 + 127 - 7
    else:
        mant, ex = np.frexp(amax / 6.0)
        byte = np.where(mant > 0.5, ex, ex - 1) + 127
    byte = np.clip(np.where(amax > 0, byte, 1), 1, 254)
    scaled = (w * np.exp2(127.0 - byte)[:, None, :]).reshape(k, n).astype(np.float32)
    by_word = np.ascontiguousarray(scaled.reshape(k // 512, 128, 4, n).transpose(0, 1, 3, 2))
    if fmt == "e4m3":
        words = by_word.astype(ml_dtypes.float8_e4m3fn).view(np.uint8)
    else:
        c = by_word.astype(ml_dtypes.float4_e2m1fn).view(np.uint8) & 0xF
        words = (c[..., 0::2] | (c[..., 1::2] << 4)).reshape(k // 512, 128, 2 * n)
    return np.ascontiguousarray(words), np.ascontiguousarray(byte.astype(np.uint8).reshape(k // 512, 16, n))


def unpack_weight(words, scales, fmt):
    g, _, n = scales.shape
    words = np.ascontiguousarray(words).reshape(g, 128, n, -1)
    if fmt == "e4m3":
        vals = words.view(ml_dtypes.float8_e4m3fn).astype(np.float64)
    else:
        nib = np.empty((g, 128, n, 4), np.uint8)
        nib[..., 0::2] = words & 0xF
        nib[..., 1::2] = words >> 4
        vals = E2M1[nib]
    vals = vals * np.repeat(np.exp2(scales.astype(np.float64) - 127.0), 8, axis=1)[..., None]
    return vals.transpose(0, 1, 3, 2).reshape(g * 512, n)


def softplus(v):
    return np.log(1.0 + np.exp(v))


def sigmoid(v):
    return 1.0 / (1.0 + np.exp(-v))


D, E, T, I, Q, G = 512, 512, 2048, 512, 128, 64


def setup_inputs():
    n = np.random.standard_normal
    idx = np.random.permutation(T)[:I]
    fd = mx_kscale(D)
    fe = mx_kscale(E)
    keysp = pack_weight(n((D, T)) / fd[:, None], "e4m3")
    valsp = pack_weight(n((E, T)) / fe[:, None], "e4m3")
    return {
        "query": (n((D, Q)) * 0.8 / np.sqrt(D) * fd[:, None]).astype(np.float32),
        "query2": (n((D, Q)) * 1.0 / np.sqrt(D) * fd[:, None]).astype(np.float32),
        "keys_words": keysp[0],
        "keys_scales": keysp[1],
        "reserve": (np.random.uniform(2.0, 10.0, (Q, 1))).astype(np.float32),
        "gout": (n((E, Q)) * 1 / np.sqrt(E) * fe[:, None]).astype(np.float32),
        "vals_words": valsp[0],
        "vals_scales": valsp[1],
        "old": (0.5 * n((Q, T))).astype(np.float32),
        "offs": striped(idx),
    }


def reference(query, query2, keys_words, keys_scales, reserve, gout, vals_words, vals_scales, old, offs):
    idx = unstriped(offs)
    keysu = unpack_weight(keys_words, keys_scales, "e4m3")
    valsu = unpack_weight(vals_words, vals_scales, "e4m3")
    queryq = mxq(f64(query), 0, "e4m3")
    keysidxg = keysu[:, idx]
    a = queryq.T @ keysidxg
    query2q = mxq(f64(query2), 0, "e4m3")
    b = query2q.T @ keysidxg
    m1 = b.reshape(Q, G, I // G).mean(axis=2)
    q0 = softplus(m1 * 3.0)
    z = np.sum(q0, axis=1, keepdims=True) + f64(reserve)
    pa = np.exp(a)
    s = pa.reshape(Q, G, I // G).sum(axis=2)
    goutq = mxq(f64(gout), 0, "e4m3")
    valsidxg = valsu[:, idx]
    c0 = goutq.T @ valsidxg
    drr = c0 * pa
    dr = drr.reshape(Q, G, I // G).sum(axis=2)
    dz = np.sum(dr * q0 / s / np.square(z) * (-1.0), axis=1, keepdims=True)
    dq0 = dr / z / s + dz
    dm1 = dq0 * sigmoid(m1 * 3.0) * 3.0
    e1 = dm1 / 8.0
    r1 = np.repeat(e1, I // G, axis=1)
    gs = r1 * 1024.0
    gf = np.zeros((Q, T))
    gf[:, idx] = gs
    y = f64(old) + gf
    return y

@@ -1,0 +1,175 @@
+from contextlib import ExitStack
+
+import concourse.mybir as mybir
+
+F32 = mybir.dt.float32
+BF16 = mybir.dt.bfloat16
+I32 = mybir.dt.int32
+U32 = mybir.dt.uint32
+U16 = mybir.dt.uint16
+U8 = mybir.dt.uint8
+FP8X4 = mybir.dt.float8_e4m3fn_x4
+ACT = mybir.ActivationFunctionType
+ALU = mybir.AluOpType
+AX = mybir.AxisListType
+
+P = 128
+PACK = 4
+Q = 128
+T = 2048
+SLOTS = 512
+PAGE = 8
+PAGES = SLOTS // PAGE
+OUT_CHUNK = 512
+
+FLOPS = 3 * 2 * 512 * Q * SLOTS
+
+
+def tile_attend_bpagequotas_s_kernel(tc, query, query2, keys_words, keys_scales, reserve, gout,
+                                      vals_words, vals_scales, old, offs, out):
+    nc = tc.nc
+    with ExitStack() as ctx:
+        sb = ctx.enter_context(tc.tile_pool(name="sb", bufs=1))
+        ps = ctx.enter_context(tc.psum_pool(name="ps", bufs=1))
+
+        offsets = sb.tile([P, SLOTS // 16], U16, name="offsets")
+        k_scale_pool = sb.tile([P, T], U8, name="k_scale_pool", align_bytes=64)
+        v_scale_pool = sb.tile([P, T], U8, name="v_scale_pool", align_bytes=64)
+        k_word_pool = sb.tile([P, T], U32, name="k_word_pool", align_bytes=64)
+        v_word_pool = sb.tile([P, T], U32, name="v_word_pool", align_bytes=64)
+        placed = sb.tile([P, T], F32, name="placed", align_bytes=64)
+        old_sb = sb.tile([P, T], F32, name="old_sb", align_bytes=64)
+        reserve_sb = sb.tile([P, 1], F32, name="reserve_sb")
+
+        nc.vector.memset(k_scale_pool[:].bitcast(I32), 0)
+        nc.vector.memset(v_scale_pool[:].bitcast(I32), 0)
+        nc.vector.memset(placed[:], 0.0)
+
+        def load_scales(pool_tile, scales):
+            for quad in range(4):
+                nc.sync.dma_start(pool_tile[:].bitcast(I32)[32 * quad:32 * quad + 4, :],
+                                  scales[0, 4 * quad:4 * quad + 4, :].bitcast(I32))
+
+        def load_words(pool_tile, words):
+            nc.scalar.dma_start(pool_tile[:].bitcast(I32), words[0].rearrange("p n t -> p (n t)").bitcast(I32))
+
+        def load_rows(name, src):
+            raw = sb.tile([P, PACK, Q], F32, name=name, align_bytes=64)
+            nc.scalar.dma_start(raw[:], src.rearrange("(p j) w -> p j w", j=PACK))
+            return raw
+
+        nc.sync.dma_start(offsets[:], offs)
+        load_scales(k_scale_pool, keys_scales)
+        load_words(k_word_pool, keys_words)
+        q2_raw = load_rows("q2_raw", query2)
+        q_raw = load_rows("q_raw", query)
+        load_scales(v_scale_pool, vals_scales)
+        warm_in = sb.tile([P, 1], F32, name="warm_in")
+        warm_out = sb.tile([P, 1], F32, name="warm_out")
+        nc.gpsimd.memset(warm_in[:], 0.0)
+        nc.scalar.activation(warm_out[:], warm_in[:], ACT.Exp)
+        load_words(v_word_pool, vals_words)
+        g_raw = load_rows("g_raw", gout)
+        nc.scalar.dma_start(reserve_sb[:], reserve)
+        nc.scalar.dma_start(old_sb[:], old)
+
+        def interleave(name, raw):
+            grouped = sb.tile([P, Q, PACK], BF16, name=name, align_bytes=64)
+            nc.scalar.activation(grouped[:], raw[:].rearrange("p j w -> p w j"), ACT.Copy)
+            return grouped
+
+        def quantize(name, grouped):
+            codes = sb.tile([P, Q], U32, name=name + "_codes", align_bytes=64)
+            scales = sb.tile([P, Q], U8, name=name + "_scales", align_bytes=64)
+            nc.vector.quantize_mx(codes[:].bitcast(FP8X4), scales[:], grouped[:].rearrange("p w j -> p (w j)"))
+            return codes, scales
+
+        def gather(name, pool_tile, dtype):
+            picked = sb.tile([P, SLOTS], dtype, name=name, align_bytes=64)
+            nc.vector.tensor_copy(picked[:], pool_tile[:].indirect(offsets[:]))
+            return picked
+
+        def scores(name, rows, words, scales):
+            acc = ps.tile([P, SLOTS], F32, name=name)
+            nc.tensor.matmul_mx(acc[:], lhsT=rows[0][:].bitcast(FP8X4), lhsT_scale=rows[1][:],
+                                rhs=words[:].bitcast(FP8X4), rhs_scale=scales[:], start=True, stop=True)
+            return acc
+
+        def small(name):
+            return sb.tile([P, PAGES], F32, name=name)
+
+        def column(name):
+            return sb.tile([P, 1], F32, name=name)
+
+        def by_page(ap):
+            return ap.rearrange("p (g j) -> p g j", j=PAGE)
+
+        def spread(ap):
+            return ap.unsqueeze(2).to_broadcast([P, PAGES, PAGE])
+
+        q2_bf = interleave("q2_bf", q2_raw)
+        q_bf = interleave("q_bf", q_raw)
+        g_bf = interleave("g_bf", g_raw)
+
+        k_scales = gather("k_scales", k_scale_pool, U8)
+        k_words = gather("k_words", k_word_pool, U32)
+        q2_mx = quantize("q2", q2_bf)
+        q_mx = quantize("q", q_bf)
+        b_ps = scores("b_ps", q2_mx, k_words, k_scales)
+        a_ps = scores("a_ps", q_mx, k_words, k_scales)
+
+        b_sum = small("b_sum")
+        nc.vector.tensor_reduce(b_sum[:], by_page(b_ps[:]), AX.X, ALU.add)
+        v_scales = gather("v_scales", v_scale_pool, U8)
+        g_mx = quantize("g", g_bf)
+
+        pa = sb.tile([P, SLOTS], F32, name="pa", align_bytes=64)
+        nc.scalar.activation(pa[:], a_ps[:], ACT.Exp)
+        x_abs = small("x_abs")
+        nc.scalar.activation(x_abs[:], b_sum[:], ACT.Abs, scale=3.0 / PAGE)
+        x_exp = small("x_exp")
+        nc.scalar.activation(x_exp[:], x_abs[:], ACT.Exp, scale=-1.0)
+        x_tanh = small("x_tanh")
+        nc.scalar.activation(x_tanh[:], b_sum[:], ACT.Tanh, scale=1.5 / PAGE)
+        x_log = small("x_log")
+        nc.scalar.activation(x_log[:], x_exp[:], ACT.Ln, bias=1.0)
+        x_pos = small("x_pos")
+        nc.scalar.activation(x_pos[:], b_sum[:], ACT.Relu, scale=3.0 / PAGE)
+
+        v_words = gather("v_words", v_word_pool, U32)
+        c_ps = scores("c_ps", g_mx, v_words, v_scales)
+
+        s = small("s")
+        nc.vector.tensor_reduce(s[:], by_page(pa[:]), AX.X, ALU.add)
+        inv_s = small("inv_s")
+        nc.vector.reciprocal(inv_s[:], s[:])
+        drr = sb.tile([P, SLOTS], F32, name="drr", align_bytes=64)
+        nc.vector.tensor_tensor(drr[:], c_ps[:], pa[:], ALU.mult)
+        slope = small("slope")
+        nc.vector.scalar_tensor_tensor(slope[:], x_tanh[:], 1.0, inv_s[:], ALU.add, ALU.mult)
+        dr = small("dr")
+        nc.vector.tensor_reduce(dr[:], by_page(drr[:]), AX.X, ALU.add)
+
+        quota = small("quota")
+        quota_sum = column("quota_sum")
+        nc.vector.scalar_tensor_tensor(quota[:], x_pos[:], 1.0, x_log[:], ALU.mult, ALU.add, accum_out=quota_sum[:])
+        z_scaled = column("z_scaled")
+        nc.vector.tensor_scalar(z_scaled[:], quota_sum[:], reserve_sb[:], -1.0 / 192.0, ALU.add, ALU.mult)
+        share = small("share")
+        nc.vector.scalar_tensor_tensor(share[:], quota[:], -1.0 / 192.0, inv_s[:], ALU.mult, ALU.mult)
+        gain = column("gain")
+        nc.vector.reciprocal(gain[:], z_scaled[:])
+        weight = sb.tile([P, SLOTS], F32, name="weight", align_bytes=64)
+        nc.scalar.activation(by_page(weight[:]), spread(slope[:]), ACT.Copy, scale=gain[:])
+        terms = small("terms")
+        centre = column("centre")
+        nc.vector.scalar_tensor_tensor(terms[:], dr[:], gain[:], share[:], ALU.mult, ALU.mult, accum_out=centre[:])
+        resid = sb.tile([P, SLOTS], F32, name="resid", align_bytes=64)
+        nc.vector.scalar_tensor_tensor(by_page(resid[:]), spread(s[:]), centre[:], spread(dr[:]), ALU.mult, ALU.subtract)
+        nc.vector.tensor_tensor(placed[:].indirect(offsets[:]), resid[:], weight[:], ALU.mult)
+
+        for c in range(T // OUT_CHUNK):
+            cols = slice(c * OUT_CHUNK, (c + 1) * OUT_CHUNK)
+            res = sb.tile([P, OUT_CHUNK], F32, name="res%d" % c, align_bytes=64)
+            nc.vector.tensor_tensor(res[:], placed[:, cols], old_sb[:, cols], ALU.add)
+            nc.sync.dma_start(out[:, cols], res[:])

@@ -20,7 +20,7 @@ T = 2048
 SLOTS = 512
 PAGE = 8
 PAGES = SLOTS // PAGE
-OUT_CHUNK = 512
+HALF = SLOTS // 2
 
 FLOPS = 3 * 2 * 512 * Q * SLOTS
 
@@ -30,15 +30,15 @@ def tile_attend_bpagequotas_s_kernel(tc, query, query2, keys_words, keys_scales,
     nc = tc.nc
     with ExitStack() as ctx:
         sb = ctx.enter_context(tc.tile_pool(name="sb", bufs=1))
+        reuse = ctx.enter_context(tc.tile_pool(name="reuse", bufs=1))
         ps = ctx.enter_context(tc.psum_pool(name="ps", bufs=1))
 
         offsets = sb.tile([P, SLOTS // 16], U16, name="offsets")
-        k_scale_pool = sb.tile([P, T], U8, name="k_scale_pool", align_bytes=64)
-        v_scale_pool = sb.tile([P, T], U8, name="v_scale_pool", align_bytes=64)
+        k_scale_pool = reuse.tile([P, T], U8, name="k_scale_pool", align_bytes=64, offset=11264)
+        v_scale_pool = reuse.tile([P, T], U8, name="v_scale_pool", align_bytes=64, offset=9216)
         k_word_pool = sb.tile([P, T], U32, name="k_word_pool", align_bytes=64)
-        v_word_pool = sb.tile([P, T], U32, name="v_word_pool", align_bytes=64)
+        v_word_pool = reuse.tile([P, T], U32, name="v_word_pool", align_bytes=64, offset=0)
         placed = sb.tile([P, T], F32, name="placed", align_bytes=64)
-        old_sb = sb.tile([P, T], F32, name="old_sb", align_bytes=64)
         reserve_sb = sb.tile([P, 1], F32, name="reserve_sb")
 
         nc.vector.memset(k_scale_pool[:].bitcast(I32), 0)
@@ -54,38 +54,34 @@ def tile_attend_bpagequotas_s_kernel(tc, query, query2, keys_words, keys_scales,
             nc.scalar.dma_start(pool_tile[:].bitcast(I32), words[0].rearrange("p n t -> p (n t)").bitcast(I32))
 
         def load_rows(name, src):
-            raw = sb.tile([P, PACK, Q], F32, name=name, align_bytes=64)
+            raw = sb.tile([P, PACK, Q], F32, name=name, tag=name, align_bytes=64)
             nc.scalar.dma_start(raw[:], src.rearrange("(p j) w -> p j w", j=PACK))
             return raw
 
         nc.sync.dma_start(offsets[:], offs)
         load_scales(k_scale_pool, keys_scales)
-        load_words(k_word_pool, keys_words)
         q2_raw = load_rows("q2_raw", query2)
-        q_raw = load_rows("q_raw", query)
+        load_words(k_word_pool, keys_words)
         load_scales(v_scale_pool, vals_scales)
         warm_in = sb.tile([P, 1], F32, name="warm_in")
         warm_out = sb.tile([P, 1], F32, name="warm_out")
         nc.gpsimd.memset(warm_in[:], 0.0)
         nc.scalar.activation(warm_out[:], warm_in[:], ACT.Exp)
-        load_words(v_word_pool, vals_words)
+        q_raw = load_rows("q_raw", query)
         g_raw = load_rows("g_raw", gout)
-        nc.scalar.dma_start(reserve_sb[:], reserve)
-        nc.scalar.dma_start(old_sb[:], old)
+        load_words(v_word_pool, vals_words)
+        nc.gpsimd.dma_start(reserve_sb[:], reserve)
 
-        def interleave(name, raw):
-            grouped = sb.tile([P, Q, PACK], BF16, name=name, align_bytes=64)
+        def interleave(grouped, raw):
             nc.scalar.activation(grouped[:], raw[:].rearrange("p j w -> p w j"), ACT.Copy)
             return grouped
 
-        def quantize(name, grouped):
-            codes = sb.tile([P, Q], U32, name=name + "_codes", align_bytes=64)
+        def quantize(name, grouped, codes):
             scales = sb.tile([P, Q], U8, name=name + "_scales", align_bytes=64)
             nc.vector.quantize_mx(codes[:].bitcast(FP8X4), scales[:], grouped[:].rearrange("p w j -> p (w j)"))
             return codes, scales
 
-        def gather(name, pool_tile, dtype):
-            picked = sb.tile([P, SLOTS], dtype, name=name, align_bytes=64)
+        def gather(picked, pool_tile):
             nc.vector.tensor_copy(picked[:], pool_tile[:].indirect(offsets[:]))
             return picked
 
@@ -105,71 +101,88 @@ def tile_attend_bpagequotas_s_kernel(tc, query, query2, keys_words, keys_scales,
             return ap.rearrange("p (g j) -> p g j", j=PAGE)
 
         def spread(ap):
-            return ap.unsqueeze(2).to_broadcast([P, PAGES, PAGE])
+            return ap.unsqueeze(2).to_broadcast([P, ap.shape[1], PAGE])
 
-        q2_bf = interleave("q2_bf", q2_raw)
-        q_bf = interleave("q_bf", q_raw)
-        g_bf = interleave("g_bf", g_raw)
+        q2_bf = interleave(sb.tile([P, Q, PACK], BF16, name="q2_bf", align_bytes=64), q2_raw)
+        q_bf = interleave(sb.tile([P, Q, PACK], BF16, name="q_bf", tag="after_q", align_bytes=64), q_raw)
+        g_bf = interleave(sb.tile([P, Q, PACK], BF16, name="g_bf", align_bytes=64), g_raw)
 
-        k_scales = gather("k_scales", k_scale_pool, U8)
-        k_words = gather("k_words", k_word_pool, U32)
-        q2_mx = quantize("q2", q2_bf)
-        q_mx = quantize("q", q_bf)
+        k_scales = gather(sb.tile([P, SLOTS], U8, name="k_scales", align_bytes=64), k_scale_pool)
+        q2_mx = quantize("q2", q2_bf, reuse.tile([P, Q], U32, name="q2_codes", align_bytes=64, offset=11264))
+        k_words = gather(reuse.tile([P, SLOTS], U32, name="k_words", align_bytes=64, offset=11264 + 1024), k_word_pool)
+        q_mx = quantize("q", q_bf, reuse.tile([P, Q], U32, name="q_codes", align_bytes=64, offset=11264 + 512))
         b_ps = scores("b_ps", q2_mx, k_words, k_scales)
         a_ps = scores("a_ps", q_mx, k_words, k_scales)
 
-        b_sum = small("b_sum")
+        v_scales = gather(sb.tile([P, SLOTS], U8, name="v_scales", tag="after_q", align_bytes=64), v_scale_pool)
+        g_mx = quantize("g", g_bf, sb.tile([P, Q], U32, name="g_codes", align_bytes=64))
+        b_sum = reuse.tile([P, PAGES], F32, name="b_sum", align_bytes=64, offset=9216)
         nc.vector.tensor_reduce(b_sum[:], by_page(b_ps[:]), AX.X, ALU.add)
-        v_scales = gather("v_scales", v_scale_pool, U8)
-        g_mx = quantize("g", g_bf)
 
         pa = sb.tile([P, SLOTS], F32, name="pa", align_bytes=64)
         nc.scalar.activation(pa[:], a_ps[:], ACT.Exp)
-        x_abs = small("x_abs")
+        x_abs = sb.tile([P, PAGES], F32, name="x_abs", tag="after_abs", align_bytes=64)
         nc.scalar.activation(x_abs[:], b_sum[:], ACT.Abs, scale=3.0 / PAGE)
         x_exp = small("x_exp")
         nc.scalar.activation(x_exp[:], x_abs[:], ACT.Exp, scale=-1.0)
         x_tanh = small("x_tanh")
         nc.scalar.activation(x_tanh[:], b_sum[:], ACT.Tanh, scale=1.5 / PAGE)
-        x_log = small("x_log")
-        nc.scalar.activation(x_log[:], x_exp[:], ACT.Ln, bias=1.0)
         x_pos = small("x_pos")
         nc.scalar.activation(x_pos[:], b_sum[:], ACT.Relu, scale=3.0 / PAGE)
+        x_log = small("x_log")
+        nc.scalar.activation(x_log[:], x_exp[:], ACT.Ln, bias=1.0)
 
-        v_words = gather("v_words", v_word_pool, U32)
-        c_ps = scores("c_ps", g_mx, v_words, v_scales)
-
-        s = small("s")
+        s = reuse.tile([P, PAGES], F32, name="s", align_bytes=64, offset=9216 + 256)
         nc.vector.tensor_reduce(s[:], by_page(pa[:]), AX.X, ALU.add)
-        inv_s = small("inv_s")
+        v_words = sb.tile([P, SLOTS], U32, name="v_words", tag="after_abs", align_bytes=64)
+        halves = [slice(h * HALF, (h + 1) * HALF) for h in range(2)]
+        page_halves = [slice(h * PAGES // 2, (h + 1) * PAGES // 2) for h in range(2)]
+        list_halves = [slice(h * HALF // 16, (h + 1) * HALF // 16) for h in range(2)]
+        c_ps = []
+        for h in range(2):
+            nc.vector.tensor_copy(v_words[:, halves[h]], v_word_pool[:].indirect(offsets[:, list_halves[h]]))
+            acc = ps.tile([P, HALF], F32, name="c_ps%d" % h)
+            nc.tensor.matmul_mx(acc[:], lhsT=g_mx[0][:].bitcast(FP8X4), lhsT_scale=g_mx[1][:],
+                                rhs=v_words[:, halves[h]].bitcast(FP8X4), rhs_scale=v_scales[:, halves[h]],
+                                start=True, stop=True)
+            c_ps.append(acc)
+        old_sb = reuse.tile([P, T], F32, name="old_sb", align_bytes=64, offset=512)
+        nc.sync.dma_start(old_sb[:], old)
+        inv_s = reuse.tile([P, PAGES], F32, name="inv_s", align_bytes=64, offset=0)
         nc.vector.reciprocal(inv_s[:], s[:])
-        drr = sb.tile([P, SLOTS], F32, name="drr", align_bytes=64)
-        nc.vector.tensor_tensor(drr[:], c_ps[:], pa[:], ALU.mult)
-        slope = small("slope")
-        nc.vector.scalar_tensor_tensor(slope[:], x_tanh[:], 1.0, inv_s[:], ALU.add, ALU.mult)
-        dr = small("dr")
-        nc.vector.tensor_reduce(dr[:], by_page(drr[:]), AX.X, ALU.add)
-
-        quota = small("quota")
+        quota = reuse.tile([P, PAGES], F32, name="quota", align_bytes=64, offset=256)
         quota_sum = column("quota_sum")
         nc.vector.scalar_tensor_tensor(quota[:], x_pos[:], 1.0, x_log[:], ALU.mult, ALU.add, accum_out=quota_sum[:])
+        slope = small("slope")
+        nc.vector.scalar_tensor_tensor(slope[:], x_tanh[:], 1.0, inv_s[:], ALU.add, ALU.mult)
         z_scaled = column("z_scaled")
         nc.vector.tensor_scalar(z_scaled[:], quota_sum[:], reserve_sb[:], -1.0 / 192.0, ALU.add, ALU.mult)
-        share = small("share")
-        nc.vector.scalar_tensor_tensor(share[:], quota[:], -1.0 / 192.0, inv_s[:], ALU.mult, ALU.mult)
+        drr = sb.tile([P, SLOTS], F32, name="drr", align_bytes=64)
+        for h in range(2):
+            nc.vector.tensor_tensor(drr[:, halves[h]], c_ps[h][:], pa[:, halves[h]], ALU.mult)
         gain = column("gain")
         nc.vector.reciprocal(gain[:], z_scaled[:])
+        share = small("share")
+        nc.vector.scalar_tensor_tensor(share[:], quota[:], -1.0 / 192.0, inv_s[:], ALU.mult, ALU.mult)
+        dr = small("dr")
+        for h in range(2):
+            nc.vector.tensor_reduce(dr[:, page_halves[h]], by_page(drr[:, halves[h]]), AX.X, ALU.add)
         weight = sb.tile([P, SLOTS], F32, name="weight", align_bytes=64)
         nc.scalar.activation(by_page(weight[:]), spread(slope[:]), ACT.Copy, scale=gain[:])
         terms = small("terms")
         centre = column("centre")
         nc.vector.scalar_tensor_tensor(terms[:], dr[:], gain[:], share[:], ALU.mult, ALU.mult, accum_out=centre[:])
         resid = sb.tile([P, SLOTS], F32, name="resid", align_bytes=64)
-        nc.vector.scalar_tensor_tensor(by_page(resid[:]), spread(s[:]), centre[:], spread(dr[:]), ALU.mult, ALU.subtract)
-        nc.vector.tensor_tensor(placed[:].indirect(offsets[:]), resid[:], weight[:], ALU.mult)
+        for h in range(2):
+            nc.vector.scalar_tensor_tensor(by_page(resid[:, halves[h]]), spread(s[:, page_halves[h]]), centre[:],
+                                           spread(dr[:, page_halves[h]]), ALU.mult, ALU.subtract)
+        for h in range(2):
+            nc.vector.tensor_tensor(placed[:].indirect(offsets[:, list_halves[h]]), resid[:, halves[h]],
+                                    weight[:, halves[h]], ALU.mult)
 
-        for c in range(T // OUT_CHUNK):
-            cols = slice(c * OUT_CHUNK, (c + 1) * OUT_CHUNK)
-            res = sb.tile([P, OUT_CHUNK], F32, name="res%d" % c, align_bytes=64)
+        edges = [0, 256, 768, 1280, 1792, T]
+        for c in range(len(edges) - 1):
+            cols = slice(edges[c], edges[c + 1])
+            res = sb.tile([P, edges[c + 1] - edges[c]], F32, name="res%d" % c, align_bytes=64)
             nc.vector.tensor_tensor(res[:], placed[:, cols], old_sb[:, cols], ALU.add)
             nc.sync.dma_start(out[:, cols], res[:])

@@ -21,6 +21,7 @@ SLOTS = 512
 PAGE = 8
 PAGES = SLOTS // PAGE
 HALF = SLOTS // 2
+V_PLANE = 4
 
 FLOPS = 3 * 2 * 512 * Q * SLOTS
 
@@ -34,45 +35,48 @@ def tile_attend_bpagequotas_s_kernel(tc, query, query2, keys_words, keys_scales,
         ps = ctx.enter_context(tc.psum_pool(name="ps", bufs=1))
 
         offsets = sb.tile([P, SLOTS // 16], U16, name="offsets")
-        k_scale_pool = reuse.tile([P, T], U8, name="k_scale_pool", align_bytes=64, offset=11264)
-        v_scale_pool = reuse.tile([P, T], U8, name="v_scale_pool", align_bytes=64, offset=9216)
+        k_scale_pool = sb.tile([P, T], U8, name="k_scale_pool", align_bytes=64)
+        v_scale_pool = sb.tile([P, T], U8, name="v_scale_pool", align_bytes=64)
         k_word_pool = sb.tile([P, T], U32, name="k_word_pool", align_bytes=64)
         v_word_pool = reuse.tile([P, T], U32, name="v_word_pool", align_bytes=64, offset=0)
         placed = sb.tile([P, T], F32, name="placed", align_bytes=64)
+        old_sb = sb.tile([P, T], F32, name="old_sb", align_bytes=64)
         reserve_sb = sb.tile([P, 1], F32, name="reserve_sb")
 
         nc.vector.memset(k_scale_pool[:].bitcast(I32), 0)
         nc.vector.memset(v_scale_pool[:].bitcast(I32), 0)
         nc.vector.memset(placed[:], 0.0)
 
-        def load_scales(pool_tile, scales):
-            for quad in range(4):
-                nc.sync.dma_start(pool_tile[:].bitcast(I32)[32 * quad:32 * quad + 4, :],
-                                  scales[0, 4 * quad:4 * quad + 4, :].bitcast(I32))
+        def load_scales(pool_tile, scales, first):
+            for r in range(4):
+                nc.sync.dma_start(pool_tile[:].bitcast(I32)[first + r:P:32, :],
+                                  scales[0, r:16:4, :].bitcast(I32))
 
         def load_words(pool_tile, words):
-            nc.scalar.dma_start(pool_tile[:].bitcast(I32), words[0].rearrange("p n t -> p (n t)").bitcast(I32))
+            nc.sync.dma_start(pool_tile[:].bitcast(I32), words[0].rearrange("p n t -> p (n t)").bitcast(I32))
 
         def load_rows(name, src):
             raw = sb.tile([P, PACK, Q], F32, name=name, tag=name, align_bytes=64)
-            nc.scalar.dma_start(raw[:], src.rearrange("(p j) w -> p j w", j=PACK))
+            nc.sync.dma_start(raw[:], src.rearrange("(p j) w -> p j w", j=PACK))
             return raw
 
+        load_scales(k_scale_pool, keys_scales, 0)
         nc.sync.dma_start(offsets[:], offs)
-        load_scales(k_scale_pool, keys_scales)
         q2_raw = load_rows("q2_raw", query2)
+        q_raw = load_rows("q_raw", query)
+        nc.sync.dma_start(reserve_sb[:], reserve)
         load_words(k_word_pool, keys_words)
-        load_scales(v_scale_pool, vals_scales)
+        g_raw = load_rows("g_raw", gout)
+        load_scales(v_scale_pool, vals_scales, V_PLANE)
+        load_words(v_word_pool, vals_words)
+        nc.sync.dma_start(old_sb[:], old)
         warm_in = sb.tile([P, 1], F32, name="warm_in")
         warm_out = sb.tile([P, 1], F32, name="warm_out")
         nc.gpsimd.memset(warm_in[:], 0.0)
         nc.scalar.activation(warm_out[:], warm_in[:], ACT.Exp)
-        q_raw = load_rows("q_raw", query)
-        g_raw = load_rows("g_raw", gout)
-        load_words(v_word_pool, vals_words)
-        nc.gpsimd.dma_start(reserve_sb[:], reserve)
 
-        def interleave(grouped, raw):
+        def interleave(name, raw):
+            grouped = sb.tile([P, Q, PACK], BF16, name=name, align_bytes=64)
             nc.scalar.activation(grouped[:], raw[:].rearrange("p j w -> p w j"), ACT.Copy)
             return grouped
 
@@ -103,82 +107,89 @@ def tile_attend_bpagequotas_s_kernel(tc, query, query2, keys_words, keys_scales,
         def spread(ap):
             return ap.unsqueeze(2).to_broadcast([P, ap.shape[1], PAGE])
 
-        q2_bf = interleave(sb.tile([P, Q, PACK], BF16, name="q2_bf", align_bytes=64), q2_raw)
-        q_bf = interleave(sb.tile([P, Q, PACK], BF16, name="q_bf", tag="after_q", align_bytes=64), q_raw)
-        g_bf = interleave(sb.tile([P, Q, PACK], BF16, name="g_bf", align_bytes=64), g_raw)
+        q2_bf = interleave("q2_bf", q2_raw)
+        q_bf = interleave("q_bf", q_raw)
+        g_bf = interleave("g_bf", g_raw)
 
+        halves = [slice(h * HALF, (h + 1) * HALF) for h in range(2)]
+        page_halves = [slice(h * PAGES // 2, (h + 1) * PAGES // 2) for h in range(2)]
+        list_halves = [slice(h * HALF // 16, (h + 1) * HALF // 16) for h in range(2)]
+
+        def half_scores(name, rows, words, scales):
+            acc = ps.tile([P, HALF], F32, name=name)
+            nc.tensor.matmul_mx(acc[:], lhsT=rows[0][:].bitcast(FP8X4), lhsT_scale=rows[1][:],
+                                rhs=words.bitcast(FP8X4), rhs_scale=scales, start=True, stop=True)
+            return acc
+
+        q2_mx = quantize("q2", q2_bf, sb.tile([P, Q], U32, name="q2_codes", align_bytes=64))
+        q_mx = quantize("q", q_bf, sb.tile([P, Q], U32, name="q_codes", align_bytes=64))
         k_scales = gather(sb.tile([P, SLOTS], U8, name="k_scales", align_bytes=64), k_scale_pool)
-        q2_mx = quantize("q2", q2_bf, reuse.tile([P, Q], U32, name="q2_codes", align_bytes=64, offset=11264))
-        k_words = gather(reuse.tile([P, SLOTS], U32, name="k_words", align_bytes=64, offset=11264 + 1024), k_word_pool)
-        q_mx = quantize("q", q_bf, reuse.tile([P, Q], U32, name="q_codes", align_bytes=64, offset=11264 + 512))
-        b_ps = scores("b_ps", q2_mx, k_words, k_scales)
+        k_words = sb.tile([P, SLOTS], U32, name="k_words", align_bytes=64)
+        b_ps = []
+        for h in range(2):
+            nc.vector.tensor_copy(k_words[:, halves[h]], k_word_pool[:].indirect(offsets[:, list_halves[h]]))
+            b_ps.append(half_scores("b_ps%d" % h, q2_mx, k_words[:, halves[h]], k_scales[:, halves[h]]))
         a_ps = scores("a_ps", q_mx, k_words, k_scales)
-
-        v_scales = gather(sb.tile([P, SLOTS], U8, name="v_scales", tag="after_q", align_bytes=64), v_scale_pool)
         g_mx = quantize("g", g_bf, sb.tile([P, Q], U32, name="g_codes", align_bytes=64))
-        b_sum = reuse.tile([P, PAGES], F32, name="b_sum", align_bytes=64, offset=9216)
-        nc.vector.tensor_reduce(b_sum[:], by_page(b_ps[:]), AX.X, ALU.add)
+        b_sum = small("b_sum")
+        for h in range(2):
+            nc.vector.tensor_reduce(b_sum[:, page_halves[h]], by_page(b_ps[h][:]), AX.X, ALU.add)
+        v_scales = gather(sb.tile([P, SLOTS], U8, name="v_scales", align_bytes=64), v_scale_pool)
 
-        pa = sb.tile([P, SLOTS], F32, name="pa", align_bytes=64)
+        pa = reuse.tile([P, SLOTS], F32, name="pa", align_bytes=64, offset=8192)
         nc.scalar.activation(pa[:], a_ps[:], ACT.Exp)
-        x_abs = sb.tile([P, PAGES], F32, name="x_abs", tag="after_abs", align_bytes=64)
+        x_abs = small("x_abs")
         nc.scalar.activation(x_abs[:], b_sum[:], ACT.Abs, scale=3.0 / PAGE)
         x_exp = small("x_exp")
         nc.scalar.activation(x_exp[:], x_abs[:], ACT.Exp, scale=-1.0)
         x_tanh = small("x_tanh")
         nc.scalar.activation(x_tanh[:], b_sum[:], ACT.Tanh, scale=1.5 / PAGE)
-        x_pos = small("x_pos")
-        nc.scalar.activation(x_pos[:], b_sum[:], ACT.Relu, scale=3.0 / PAGE)
         x_log = small("x_log")
-        nc.scalar.activation(x_log[:], x_exp[:], ACT.Ln, bias=1.0)
+        log_sum = column("log_sum")
+        nc.scalar.activation(x_log[:], x_exp[:], ACT.Ln, bias=1.0, accum_out=log_sum[:])
+        x_pos = small("x_pos")
+        pos_sum = column("pos_sum")
+        nc.scalar.activation(x_pos[:], b_sum[:], ACT.Relu, scale=3.0 / PAGE, accum_out=pos_sum[:])
+        z_part = column("z_part")
+        nc.scalar.activation(z_part[:], pos_sum[:], ACT.Identity, bias=reserve_sb[:])
+        z = column("z")
+        nc.scalar.activation(z[:], log_sum[:], ACT.Identity, bias=z_part[:])
 
-        s = reuse.tile([P, PAGES], F32, name="s", align_bytes=64, offset=9216 + 256)
-        nc.vector.tensor_reduce(s[:], by_page(pa[:]), AX.X, ALU.add)
-        v_words = sb.tile([P, SLOTS], U32, name="v_words", tag="after_abs", align_bytes=64)
-        halves = [slice(h * HALF, (h + 1) * HALF) for h in range(2)]
-        page_halves = [slice(h * PAGES // 2, (h + 1) * PAGES // 2) for h in range(2)]
-        list_halves = [slice(h * HALF // 16, (h + 1) * HALF // 16) for h in range(2)]
+        weight = sb.tile([P, SLOTS], F32, name="weight", align_bytes=64)
+        nc.scalar.activation(by_page(weight[:]), spread(x_tanh[:]), ACT.Copy, scale=192.0, bias=192.0)
+        pa_pages = by_page(pa[:])
+        s4 = sb.tile([P, PAGES, 4], F32, name="s4")
+        nc.gpsimd.tensor_tensor(s4[:], pa_pages[:, :, 0:4], pa_pages[:, :, 4:8], ALU.add)
+        s2 = sb.tile([P, PAGES, 2], F32, name="s2")
+        nc.gpsimd.tensor_tensor(s2[:], s4[:, :, 0:2], s4[:, :, 2:4], ALU.add)
+        s = small("s")
+        nc.gpsimd.tensor_tensor(s[:], s2[:, :, 0], s2[:, :, 1], ALU.add)
+
+        v_words = sb.tile([P, SLOTS], U32, name="v_words", align_bytes=64)
         c_ps = []
         for h in range(2):
             nc.vector.tensor_copy(v_words[:, halves[h]], v_word_pool[:].indirect(offsets[:, list_halves[h]]))
-            acc = ps.tile([P, HALF], F32, name="c_ps%d" % h)
-            nc.tensor.matmul_mx(acc[:], lhsT=g_mx[0][:].bitcast(FP8X4), lhsT_scale=g_mx[1][:],
-                                rhs=v_words[:, halves[h]].bitcast(FP8X4), rhs_scale=v_scales[:, halves[h]],
-                                start=True, stop=True)
-            c_ps.append(acc)
-        old_sb = reuse.tile([P, T], F32, name="old_sb", align_bytes=64, offset=512)
-        nc.sync.dma_start(old_sb[:], old)
+            c_ps.append(half_scores("c_ps%d" % h, g_mx, v_words[:, halves[h]], v_scales[V_PLANE:P, halves[h]]))
         inv_s = reuse.tile([P, PAGES], F32, name="inv_s", align_bytes=64, offset=0)
-        nc.vector.reciprocal(inv_s[:], s[:])
-        quota = reuse.tile([P, PAGES], F32, name="quota", align_bytes=64, offset=256)
-        quota_sum = column("quota_sum")
-        nc.vector.scalar_tensor_tensor(quota[:], x_pos[:], 1.0, x_log[:], ALU.mult, ALU.add, accum_out=quota_sum[:])
-        slope = small("slope")
-        nc.vector.scalar_tensor_tensor(slope[:], x_tanh[:], 1.0, inv_s[:], ALU.add, ALU.mult)
-        z_scaled = column("z_scaled")
-        nc.vector.tensor_scalar(z_scaled[:], quota_sum[:], reserve_sb[:], -1.0 / 192.0, ALU.add, ALU.mult)
         drr = sb.tile([P, SLOTS], F32, name="drr", align_bytes=64)
-        for h in range(2):
-            nc.vector.tensor_tensor(drr[:, halves[h]], c_ps[h][:], pa[:, halves[h]], ALU.mult)
-        gain = column("gain")
-        nc.vector.reciprocal(gain[:], z_scaled[:])
-        share = small("share")
-        nc.vector.scalar_tensor_tensor(share[:], quota[:], -1.0 / 192.0, inv_s[:], ALU.mult, ALU.mult)
+        nc.vector.tensor_tensor(drr[:, halves[0]], c_ps[0][:], pa[:, halves[0]], ALU.mult)
+        nc.vector.reciprocal(inv_s[:], s[:])
+        nc.vector.tensor_tensor(drr[:, halves[1]], c_ps[1][:], pa[:, halves[1]], ALU.mult)
         dr = small("dr")
-        for h in range(2):
-            nc.vector.tensor_reduce(dr[:, page_halves[h]], by_page(drr[:, halves[h]]), AX.X, ALU.add)
-        weight = sb.tile([P, SLOTS], F32, name="weight", align_bytes=64)
-        nc.scalar.activation(by_page(weight[:]), spread(slope[:]), ACT.Copy, scale=gain[:])
+        nc.vector.tensor_reduce(dr[:, page_halves[0]], by_page(drr[:, halves[0]]), AX.X, ALU.add)
+        gain = reuse.tile([P, 1], F32, name="gain", align_bytes=64, offset=8192)
+        nc.vector.reciprocal(gain[:], z[:])
+        nc.vector.tensor_reduce(dr[:, page_halves[1]], by_page(drr[:, halves[1]]), AX.X, ALU.add)
+        quota = reuse.tile([P, PAGES], F32, name="quota", align_bytes=64, offset=8192 + 64)
+        nc.vector.tensor_tensor(quota[:], x_pos[:], x_log[:], ALU.add)
+        mean = small("mean")
+        nc.vector.tensor_tensor(mean[:], dr[:], inv_s[:], ALU.mult)
         terms = small("terms")
         centre = column("centre")
-        nc.vector.scalar_tensor_tensor(terms[:], dr[:], gain[:], share[:], ALU.mult, ALU.mult, accum_out=centre[:])
+        nc.vector.scalar_tensor_tensor(terms[:], mean[:], gain[:], quota[:], ALU.mult, ALU.mult, accum_out=centre[:])
         resid = sb.tile([P, SLOTS], F32, name="resid", align_bytes=64)
-        for h in range(2):
-            nc.vector.scalar_tensor_tensor(by_page(resid[:, halves[h]]), spread(s[:, page_halves[h]]), centre[:],
-                                           spread(dr[:, page_halves[h]]), ALU.mult, ALU.subtract)
-        for h in range(2):
-            nc.vector.tensor_tensor(placed[:].indirect(offsets[:, list_halves[h]]), resid[:, halves[h]],
-                                    weight[:, halves[h]], ALU.mult)
+        nc.vector.tensor_scalar(by_page(resid[:]), spread(mean[:]), centre[:], gain[:], ALU.subtract, ALU.mult)
+        nc.vector.tensor_tensor(placed[:].indirect(offsets[:]), resid[:], weight[:], ALU.mult)
 
         edges = [0, 256, 768, 1280, 1792, T]
         for c in range(len(edges) - 1):

@@ -15,15 +15,23 @@ AX = mybir.AxisListType
 
 P = 128
 PACK = 4
+K = P * PACK
 Q = 128
 T = 2048
 SLOTS = 512
 PAGE = 8
 PAGES = SLOTS // PAGE
 HALF = SLOTS // 2
-V_PLANE = 4
+LIST_ROWS = 16
+SCALE_ROWS = K // 32
+QUADRANT = 32
+V_FIRST = 4
+HALF_GAIN = 3.0 / PAGE * 1024.0 / 2.0
+PA_BYTES = 4 * T
+QUOTA_BYTES = PA_BYTES + 64
+OUT_EDGES = [0, 256, 768, 1280, 1792, T]
 
-FLOPS = 3 * 2 * 512 * Q * SLOTS
+FLOPS = 3 * 2 * K * Q * SLOTS
 
 
 def tile_attend_bpagequotas_s_kernel(tc, query, query2, keys_words, keys_scales, reserve, gout,
@@ -34,7 +42,7 @@ def tile_attend_bpagequotas_s_kernel(tc, query, query2, keys_words, keys_scales,
         reuse = ctx.enter_context(tc.tile_pool(name="reuse", bufs=1))
         ps = ctx.enter_context(tc.psum_pool(name="ps", bufs=1))
 
-        offsets = sb.tile([P, SLOTS // 16], U16, name="offsets")
+        offsets = sb.tile([P, SLOTS // LIST_ROWS], U16, name="offsets")
         k_scale_pool = sb.tile([P, T], U8, name="k_scale_pool", align_bytes=64)
         v_scale_pool = sb.tile([P, T], U8, name="v_scale_pool", align_bytes=64)
         k_word_pool = sb.tile([P, T], U32, name="k_word_pool", align_bytes=64)
@@ -49,14 +57,14 @@ def tile_attend_bpagequotas_s_kernel(tc, query, query2, keys_words, keys_scales,
 
         def load_scales(pool_tile, scales, first):
             for r in range(4):
-                nc.sync.dma_start(pool_tile[:].bitcast(I32)[first + r:P:32, :],
-                                  scales[0, r:16:4, :].bitcast(I32))
+                nc.sync.dma_start(pool_tile[:].bitcast(I32)[first + r:P:QUADRANT, :],
+                                  scales[0, r:SCALE_ROWS:4, :].bitcast(I32))
 
         def load_words(pool_tile, words):
             nc.sync.dma_start(pool_tile[:].bitcast(I32), words[0].rearrange("p n t -> p (n t)").bitcast(I32))
 
         def load_rows(name, src):
-            raw = sb.tile([P, PACK, Q], F32, name=name, tag=name, align_bytes=64)
+            raw = sb.tile([P, PACK, Q], F32, name=name, align_bytes=64)
             nc.sync.dma_start(raw[:], src.rearrange("(p j) w -> p j w", j=PACK))
             return raw
 
@@ -67,45 +75,41 @@ def tile_attend_bpagequotas_s_kernel(tc, query, query2, keys_words, keys_scales,
         nc.sync.dma_start(reserve_sb[:], reserve)
         load_words(k_word_pool, keys_words)
         g_raw = load_rows("g_raw", gout)
-        load_scales(v_scale_pool, vals_scales, V_PLANE)
+        load_scales(v_scale_pool, vals_scales, V_FIRST)
         load_words(v_word_pool, vals_words)
         nc.sync.dma_start(old_sb[:], old)
-        warm_in = sb.tile([P, 1], F32, name="warm_in")
-        warm_out = sb.tile([P, 1], F32, name="warm_out")
-        nc.gpsimd.memset(warm_in[:], 0.0)
-        nc.scalar.activation(warm_out[:], warm_in[:], ACT.Exp)
 
         def interleave(name, raw):
             grouped = sb.tile([P, Q, PACK], BF16, name=name, align_bytes=64)
             nc.scalar.activation(grouped[:], raw[:].rearrange("p j w -> p w j"), ACT.Copy)
             return grouped
 
-        def quantize(name, grouped, codes):
+        def quantize(name, grouped):
+            codes = sb.tile([P, Q], U32, name=name + "_codes", align_bytes=64)
             scales = sb.tile([P, Q], U8, name=name + "_scales", align_bytes=64)
             nc.vector.quantize_mx(codes[:].bitcast(FP8X4), scales[:], grouped[:].rearrange("p w j -> p (w j)"))
             return codes, scales
 
-        def gather(picked, pool_tile):
-            nc.vector.tensor_copy(picked[:], pool_tile[:].indirect(offsets[:]))
-            return picked
+        def gather(picked, pool_tile, entries):
+            nc.vector.tensor_copy(picked, pool_tile[:].indirect(entries))
 
         def scores(name, rows, words, scales):
-            acc = ps.tile([P, SLOTS], F32, name=name)
+            acc = ps.tile([P, words.shape[1]], F32, name=name)
             nc.tensor.matmul_mx(acc[:], lhsT=rows[0][:].bitcast(FP8X4), lhsT_scale=rows[1][:],
-                                rhs=words[:].bitcast(FP8X4), rhs_scale=scales[:], start=True, stop=True)
+                                rhs=words.bitcast(FP8X4), rhs_scale=scales, start=True, stop=True)
             return acc
 
-        def small(name):
+        def per_page(name):
             return sb.tile([P, PAGES], F32, name=name)
 
-        def column(name):
+        def per_row(name):
             return sb.tile([P, 1], F32, name=name)
 
         def by_page(ap):
             return ap.rearrange("p (g j) -> p g j", j=PAGE)
 
         def spread(ap):
-            return ap.unsqueeze(2).to_broadcast([P, ap.shape[1], PAGE])
+            return ap.unsqueeze(2).to_broadcast([P, PAGES, PAGE])
 
         q2_bf = interleave("q2_bf", q2_raw)
         q_bf = interleave("q_bf", q_raw)
@@ -113,87 +117,85 @@ def tile_attend_bpagequotas_s_kernel(tc, query, query2, keys_words, keys_scales,
 
         halves = [slice(h * HALF, (h + 1) * HALF) for h in range(2)]
         page_halves = [slice(h * PAGES // 2, (h + 1) * PAGES // 2) for h in range(2)]
-        list_halves = [slice(h * HALF // 16, (h + 1) * HALF // 16) for h in range(2)]
+        list_halves = [slice(h * HALF // LIST_ROWS, (h + 1) * HALF // LIST_ROWS) for h in range(2)]
 
-        def half_scores(name, rows, words, scales):
-            acc = ps.tile([P, HALF], F32, name=name)
-            nc.tensor.matmul_mx(acc[:], lhsT=rows[0][:].bitcast(FP8X4), lhsT_scale=rows[1][:],
-                                rhs=words.bitcast(FP8X4), rhs_scale=scales, start=True, stop=True)
-            return acc
-
-        q2_mx = quantize("q2", q2_bf, sb.tile([P, Q], U32, name="q2_codes", align_bytes=64))
-        q_mx = quantize("q", q_bf, sb.tile([P, Q], U32, name="q_codes", align_bytes=64))
-        k_scales = gather(sb.tile([P, SLOTS], U8, name="k_scales", align_bytes=64), k_scale_pool)
+        q2_mx = quantize("q2", q2_bf)
+        q_mx = quantize("q", q_bf)
+        k_scales = sb.tile([P, SLOTS], U8, name="k_scales", align_bytes=64)
+        gather(k_scales[:], k_scale_pool, offsets[:])
         k_words = sb.tile([P, SLOTS], U32, name="k_words", align_bytes=64)
         b_ps = []
         for h in range(2):
-            nc.vector.tensor_copy(k_words[:, halves[h]], k_word_pool[:].indirect(offsets[:, list_halves[h]]))
-            b_ps.append(half_scores("b_ps%d" % h, q2_mx, k_words[:, halves[h]], k_scales[:, halves[h]]))
-        a_ps = scores("a_ps", q_mx, k_words, k_scales)
-        g_mx = quantize("g", g_bf, sb.tile([P, Q], U32, name="g_codes", align_bytes=64))
-        b_sum = small("b_sum")
+            gather(k_words[:, halves[h]], k_word_pool, offsets[:, list_halves[h]])
+            b_ps.append(scores("b_ps%d" % h, q2_mx, k_words[:, halves[h]], k_scales[:, halves[h]]))
+        a_ps = scores("a_ps", q_mx, k_words[:], k_scales[:])
+        g_mx = quantize("g", g_bf)
+        b_sum = per_page("b_sum")
         for h in range(2):
             nc.vector.tensor_reduce(b_sum[:, page_halves[h]], by_page(b_ps[h][:]), AX.X, ALU.add)
-        v_scales = gather(sb.tile([P, SLOTS], U8, name="v_scales", align_bytes=64), v_scale_pool)
+        v_scales = sb.tile([P, SLOTS], U8, name="v_scales", align_bytes=64)
+        gather(v_scales[:], v_scale_pool, offsets[:])
 
-        pa = reuse.tile([P, SLOTS], F32, name="pa", align_bytes=64, offset=8192)
+        pa = reuse.tile([P, SLOTS], F32, name="pa", align_bytes=64, offset=PA_BYTES)
         nc.scalar.activation(pa[:], a_ps[:], ACT.Exp)
-        x_abs = small("x_abs")
+        x_abs = per_page("x_abs")
         nc.scalar.activation(x_abs[:], b_sum[:], ACT.Abs, scale=3.0 / PAGE)
-        x_exp = small("x_exp")
+        x_exp = per_page("x_exp")
         nc.scalar.activation(x_exp[:], x_abs[:], ACT.Exp, scale=-1.0)
-        x_tanh = small("x_tanh")
+        x_tanh = per_page("x_tanh")
         nc.scalar.activation(x_tanh[:], b_sum[:], ACT.Tanh, scale=1.5 / PAGE)
-        x_log = small("x_log")
-        log_sum = column("log_sum")
+        x_log = per_page("x_log")
+        log_sum = per_row("log_sum")
         nc.scalar.activation(x_log[:], x_exp[:], ACT.Ln, bias=1.0, accum_out=log_sum[:])
-        x_pos = small("x_pos")
-        pos_sum = column("pos_sum")
+        x_pos = per_page("x_pos")
+        pos_sum = per_row("pos_sum")
         nc.scalar.activation(x_pos[:], b_sum[:], ACT.Relu, scale=3.0 / PAGE, accum_out=pos_sum[:])
-        z_part = column("z_part")
+        z_part = per_row("z_part")
         nc.scalar.activation(z_part[:], pos_sum[:], ACT.Identity, bias=reserve_sb[:])
-        z = column("z")
+        z = per_row("z")
         nc.scalar.activation(z[:], log_sum[:], ACT.Identity, bias=z_part[:])
-
         weight = sb.tile([P, SLOTS], F32, name="weight", align_bytes=64)
-        nc.scalar.activation(by_page(weight[:]), spread(x_tanh[:]), ACT.Copy, scale=192.0, bias=192.0)
+        nc.scalar.activation(by_page(weight[:]), spread(x_tanh[:]), ACT.Copy, scale=HALF_GAIN, bias=HALF_GAIN)
+
         pa_pages = by_page(pa[:])
         s4 = sb.tile([P, PAGES, 4], F32, name="s4")
         nc.gpsimd.tensor_tensor(s4[:], pa_pages[:, :, 0:4], pa_pages[:, :, 4:8], ALU.add)
         s2 = sb.tile([P, PAGES, 2], F32, name="s2")
         nc.gpsimd.tensor_tensor(s2[:], s4[:, :, 0:2], s4[:, :, 2:4], ALU.add)
-        s = small("s")
+        s = per_page("s")
         nc.gpsimd.tensor_tensor(s[:], s2[:, :, 0], s2[:, :, 1], ALU.add)
 
         v_words = sb.tile([P, SLOTS], U32, name="v_words", align_bytes=64)
         c_ps = []
         for h in range(2):
-            nc.vector.tensor_copy(v_words[:, halves[h]], v_word_pool[:].indirect(offsets[:, list_halves[h]]))
-            c_ps.append(half_scores("c_ps%d" % h, g_mx, v_words[:, halves[h]], v_scales[V_PLANE:P, halves[h]]))
+            gather(v_words[:, halves[h]], v_word_pool, offsets[:, list_halves[h]])
+            c_ps.append(scores("c_ps%d" % h, g_mx, v_words[:, halves[h]], v_scales[V_FIRST:P, halves[h]]))
         inv_s = reuse.tile([P, PAGES], F32, name="inv_s", align_bytes=64, offset=0)
         drr = sb.tile([P, SLOTS], F32, name="drr", align_bytes=64)
         nc.vector.tensor_tensor(drr[:, halves[0]], c_ps[0][:], pa[:, halves[0]], ALU.mult)
         nc.vector.reciprocal(inv_s[:], s[:])
         nc.vector.tensor_tensor(drr[:, halves[1]], c_ps[1][:], pa[:, halves[1]], ALU.mult)
-        dr = small("dr")
-        nc.vector.tensor_reduce(dr[:, page_halves[0]], by_page(drr[:, halves[0]]), AX.X, ALU.add)
-        gain = reuse.tile([P, 1], F32, name="gain", align_bytes=64, offset=8192)
-        nc.vector.reciprocal(gain[:], z[:])
-        nc.vector.tensor_reduce(dr[:, page_halves[1]], by_page(drr[:, halves[1]]), AX.X, ALU.add)
-        quota = reuse.tile([P, PAGES], F32, name="quota", align_bytes=64, offset=8192 + 64)
+        dr = per_page("dr")
+        quota = reuse.tile([P, PAGES], F32, name="quota", align_bytes=64, offset=QUOTA_BYTES)
         nc.vector.tensor_tensor(quota[:], x_pos[:], x_log[:], ALU.add)
-        mean = small("mean")
+        nc.vector.tensor_reduce(dr[:, page_halves[0]], by_page(drr[:, halves[0]]), AX.X, ALU.add)
+        inv_z = reuse.tile([P, 1], F32, name="inv_z", align_bytes=64, offset=PA_BYTES)
+        nc.vector.reciprocal(inv_z[:], z[:])
+        share = per_page("share")
+        nc.vector.tensor_tensor(share[:], quota[:], inv_s[:], ALU.mult)
+        nc.vector.tensor_reduce(dr[:, page_halves[1]], by_page(drr[:, halves[1]]), AX.X, ALU.add)
+        terms = per_page("terms")
+        centre = per_row("centre")
+        nc.vector.scalar_tensor_tensor(terms[:], dr[:], inv_z[:], share[:], ALU.mult, ALU.mult, accum_out=centre[:])
+        mean = per_page("mean")
         nc.vector.tensor_tensor(mean[:], dr[:], inv_s[:], ALU.mult)
-        terms = small("terms")
-        centre = column("centre")
-        nc.vector.scalar_tensor_tensor(terms[:], mean[:], gain[:], quota[:], ALU.mult, ALU.mult, accum_out=centre[:])
+
         resid = sb.tile([P, SLOTS], F32, name="resid", align_bytes=64)
-        nc.vector.tensor_scalar(by_page(resid[:]), spread(mean[:]), centre[:], gain[:], ALU.subtract, ALU.mult)
+        nc.vector.tensor_scalar(by_page(resid[:]), spread(mean[:]), centre[:], inv_z[:], ALU.subtract, ALU.mult)
         nc.vector.tensor_tensor(placed[:].indirect(offsets[:]), resid[:], weight[:], ALU.mult)
 
-        edges = [0, 256, 768, 1280, 1792, T]
-        for c in range(len(edges) - 1):
-            cols = slice(edges[c], edges[c + 1])
-            res = sb.tile([P, edges[c + 1] - edges[c]], F32, name="res%d" % c, align_bytes=64)
+        for c in range(len(OUT_EDGES) - 1):
+            cols = slice(OUT_EDGES[c], OUT_EDGES[c + 1])
+            res = sb.tile([P, OUT_EDGES[c + 1] - OUT_EDGES[c]], F32, name="res%d" % c, align_bytes=64)
             nc.vector.tensor_tensor(res[:], placed[:, cols], old_sb[:, cols], ALU.add)
             nc.sync.dma_start(out[:, cols], res[:])

from contextlib import ExitStack

import concourse.mybir as mybir

F32 = mybir.dt.float32
BF16 = mybir.dt.bfloat16
I32 = mybir.dt.int32
U32 = mybir.dt.uint32
U16 = mybir.dt.uint16
U8 = mybir.dt.uint8
FP8X4 = mybir.dt.float8_e4m3fn_x4
ACT = mybir.ActivationFunctionType
ALU = mybir.AluOpType
AX = mybir.AxisListType

P = 128
PACK = 4
K = P * PACK
Q = 128
T = 2048
SLOTS = 512
PAGE = 8
PAGES = SLOTS // PAGE
HALF = SLOTS // 2
LIST_ROWS = 16
SCALE_ROWS = K // 32
QUADRANT = 32
V_FIRST = 4
HALF_GAIN = 3.0 / PAGE * 1024.0 / 2.0
PA_BYTES = 4 * T
QUOTA_BYTES = PA_BYTES + 64
OUT_EDGES = [0, 256, 768, 1280, 1792, T]

FLOPS = 3 * 2 * K * Q * SLOTS


def tile_attend_bpagequotas_s_kernel(tc, query, query2, keys_words, keys_scales, reserve, gout,
                                      vals_words, vals_scales, old, offs, out):
    nc = tc.nc
    with ExitStack() as ctx:
        sb = ctx.enter_context(tc.tile_pool(name="sb", bufs=1))
        reuse = ctx.enter_context(tc.tile_pool(name="reuse", bufs=1))
        ps = ctx.enter_context(tc.psum_pool(name="ps", bufs=1))

        offsets = sb.tile([P, SLOTS // LIST_ROWS], U16, name="offsets")
        k_scale_pool = sb.tile([P, T], U8, name="k_scale_pool", align_bytes=64)
        v_scale_pool = sb.tile([P, T], U8, name="v_scale_pool", align_bytes=64)
        k_word_pool = sb.tile([P, T], U32, name="k_word_pool", align_bytes=64)
        v_word_pool = reuse.tile([P, T], U32, name="v_word_pool", align_bytes=64, offset=0)
        placed = sb.tile([P, T], F32, name="placed", align_bytes=64)
        old_sb = sb.tile([P, T], F32, name="old_sb", align_bytes=64)
        reserve_sb = sb.tile([P, 1], F32, name="reserve_sb")

        nc.vector.memset(k_scale_pool[:].bitcast(I32), 0)
        nc.vector.memset(v_scale_pool[:].bitcast(I32), 0)
        nc.vector.memset(placed[:], 0.0)

        def load_scales(pool_tile, scales, first):
            for r in range(4):
                nc.sync.dma_start(pool_tile[:].bitcast(I32)[first + r:P:QUADRANT, :],
                                  scales[0, r:SCALE_ROWS:4, :].bitcast(I32))

        def load_words(pool_tile, words):
            nc.sync.dma_start(pool_tile[:].bitcast(I32), words[0].rearrange("p n t -> p (n t)").bitcast(I32))

        def load_rows(name, src):
            raw = sb.tile([P, PACK, Q], F32, name=name, align_bytes=64)
            nc.sync.dma_start(raw[:], src.rearrange("(p j) w -> p j w", j=PACK))
            return raw

        load_scales(k_scale_pool, keys_scales, 0)
        nc.sync.dma_start(offsets[:], offs)
        q2_raw = load_rows("q2_raw", query2)
        q_raw = load_rows("q_raw", query)
        nc.sync.dma_start(reserve_sb[:], reserve)
        load_words(k_word_pool, keys_words)
        g_raw = load_rows("g_raw", gout)
        load_scales(v_scale_pool, vals_scales, V_FIRST)
        load_words(v_word_pool, vals_words)
        nc.sync.dma_start(old_sb[:], old)

        def interleave(name, raw):
            grouped = sb.tile([P, Q, PACK], BF16, name=name, align_bytes=64)
            nc.scalar.activation(grouped[:], raw[:].rearrange("p j w -> p w j"), ACT.Copy)
            return grouped

        def quantize(name, grouped):
            codes = sb.tile([P, Q], U32, name=name + "_codes", align_bytes=64)
            scales = sb.tile([P, Q], U8, name=name + "_scales", align_bytes=64)
            nc.vector.quantize_mx(codes[:].bitcast(FP8X4), scales[:], grouped[:].rearrange("p w j -> p (w j)"))
            return codes, scales

        def gather(picked, pool_tile, entries):
            nc.vector.tensor_copy(picked, pool_tile[:].indirect(entries))

        def scores(name, rows, words, scales):
            acc = ps.tile([P, words.shape[1]], F32, name=name)
            nc.tensor.matmul_mx(acc[:], lhsT=rows[0][:].bitcast(FP8X4), lhsT_scale=rows[1][:],
                                rhs=words.bitcast(FP8X4), rhs_scale=scales, start=True, stop=True)
            return acc

        def per_page(name):
            return sb.tile([P, PAGES], F32, name=name)

        def per_row(name):
            return sb.tile([P, 1], F32, name=name)

        def by_page(ap):
            return ap.rearrange("p (g j) -> p g j", j=PAGE)

        def spread(ap):
            return ap.unsqueeze(2).to_broadcast([P, PAGES, PAGE])

        q2_bf = interleave("q2_bf", q2_raw)
        q_bf = interleave("q_bf", q_raw)
        g_bf = interleave("g_bf", g_raw)

        halves = [slice(h * HALF, (h + 1) * HALF) for h in range(2)]
        page_halves = [slice(h * PAGES // 2, (h + 1) * PAGES // 2) for h in range(2)]
        list_halves = [slice(h * HALF // LIST_ROWS, (h + 1) * HALF // LIST_ROWS) for h in range(2)]

        q2_mx = quantize("q2", q2_bf)
        q_mx = quantize("q", q_bf)
        k_scales = sb.tile([P, SLOTS], U8, name="k_scales", align_bytes=64)
        gather(k_scales[:], k_scale_pool, offsets[:])
        k_words = sb.tile([P, SLOTS], U32, name="k_words", align_bytes=64)
        b_ps = []
        for h in range(2):
            gather(k_words[:, halves[h]], k_word_pool, offsets[:, list_halves[h]])
            b_ps.append(scores("b_ps%d" % h, q2_mx, k_words[:, halves[h]], k_scales[:, halves[h]]))
        a_ps = scores("a_ps", q_mx, k_words[:], k_scales[:])
        g_mx = quantize("g", g_bf)
        b_sum = per_page("b_sum")
        for h in range(2):
            nc.vector.tensor_reduce(b_sum[:, page_halves[h]], by_page(b_ps[h][:]), AX.X, ALU.add)
        v_scales = sb.tile([P, SLOTS], U8, name="v_scales", align_bytes=64)
        gather(v_scales[:], v_scale_pool, offsets[:])

        pa = reuse.tile([P, SLOTS], F32, name="pa", align_bytes=64, offset=PA_BYTES)
        nc.scalar.activation(pa[:], a_ps[:], ACT.Exp)
        x_abs = per_page("x_abs")
        nc.scalar.activation(x_abs[:], b_sum[:], ACT.Abs, scale=3.0 / PAGE)
        x_exp = per_page("x_exp")
        nc.scalar.activation(x_exp[:], x_abs[:], ACT.Exp, scale=-1.0)
        x_tanh = per_page("x_tanh")
        nc.scalar.activation(x_tanh[:], b_sum[:], ACT.Tanh, scale=1.5 / PAGE)
        x_log = per_page("x_log")
        log_sum = per_row("log_sum")
        nc.scalar.activation(x_log[:], x_exp[:], ACT.Ln, bias=1.0, accum_out=log_sum[:])
        x_pos = per_page("x_pos")
        pos_sum = per_row("pos_sum")
        nc.scalar.activation(x_pos[:], b_sum[:], ACT.Relu, scale=3.0 / PAGE, accum_out=pos_sum[:])
        z_part = per_row("z_part")
        nc.scalar.activation(z_part[:], pos_sum[:], ACT.Identity, bias=reserve_sb[:])
        z = per_row("z")
        nc.scalar.activation(z[:], log_sum[:], ACT.Identity, bias=z_part[:])
        weight = sb.tile([P, SLOTS], F32, name="weight", align_bytes=64)
        nc.scalar.activation(by_page(weight[:]), spread(x_tanh[:]), ACT.Copy, scale=HALF_GAIN, bias=HALF_GAIN)

        pa_pages = by_page(pa[:])
        s4 = sb.tile([P, PAGES, 4], F32, name="s4")
        nc.gpsimd.tensor_tensor(s4[:], pa_pages[:, :, 0:4], pa_pages[:, :, 4:8], ALU.add)
        s2 = sb.tile([P, PAGES, 2], F32, name="s2")
        nc.gpsimd.tensor_tensor(s2[:], s4[:, :, 0:2], s4[:, :, 2:4], ALU.add)
        s = per_page("s")
        nc.gpsimd.tensor_tensor(s[:], s2[:, :, 0], s2[:, :, 1], ALU.add)

        v_words = sb.tile([P, SLOTS], U32, name="v_words", align_bytes=64)
        c_ps = []
        for h in range(2):
            gather(v_words[:, halves[h]], v_word_pool, offsets[:, list_halves[h]])
            c_ps.append(scores("c_ps%d" % h, g_mx, v_words[:, halves[h]], v_scales[V_FIRST:P, halves[h]]))
        inv_s = reuse.tile([P, PAGES], F32, name="inv_s", align_bytes=64, offset=0)
        drr = sb.tile([P, SLOTS], F32, name="drr", align_bytes=64)
        nc.vector.tensor_tensor(drr[:, halves[0]], c_ps[0][:], pa[:, halves[0]], ALU.mult)
        nc.vector.reciprocal(inv_s[:], s[:])
        nc.vector.tensor_tensor(drr[:, halves[1]], c_ps[1][:], pa[:, halves[1]], ALU.mult)
        dr = per_page("dr")
        quota = reuse.tile([P, PAGES], F32, name="quota", align_bytes=64, offset=QUOTA_BYTES)
        nc.vector.tensor_tensor(quota[:], x_pos[:], x_log[:], ALU.add)
        nc.vector.tensor_reduce(dr[:, page_halves[0]], by_page(drr[:, halves[0]]), AX.X, ALU.add)
        inv_z = reuse.tile([P, 1], F32, name="inv_z", align_bytes=64, offset=PA_BYTES)
        nc.vector.reciprocal(inv_z[:], z[:])
        share = per_page("share")
        nc.vector.tensor_tensor(share[:], quota[:], inv_s[:], ALU.mult)
        nc.vector.tensor_reduce(dr[:, page_halves[1]], by_page(drr[:, halves[1]]), AX.X, ALU.add)
        terms = per_page("terms")
        centre = per_row("centre")
        nc.vector.scalar_tensor_tensor(terms[:], dr[:], inv_z[:], share[:], ALU.mult, ALU.mult, accum_out=centre[:])
        mean = per_page("mean")
        nc.vector.tensor_tensor(mean[:], dr[:], inv_s[:], ALU.mult)

        resid = sb.tile([P, SLOTS], F32, name="resid", align_bytes=64)
        nc.vector.tensor_scalar(by_page(resid[:]), spread(mean[:]), centre[:], inv_z[:], ALU.subtract, ALU.mult)
        nc.vector.tensor_tensor(placed[:].indirect(offsets[:]), resid[:], weight[:], ALU.mult)

        for c in range(len(OUT_EDGES) - 1):
            cols = slice(OUT_EDGES[c], OUT_EDGES[c + 1])
            res = sb.tile([P, OUT_EDGES[c + 1] - OUT_EDGES[c]], F32, name="res%d" % c, align_bytes=64)
            nc.vector.tensor_tensor(res[:], placed[:, cols], old_sb[:, cols], ALU.add)
            nc.sync.dma_start(out[:, cols], res[:])
